import numpy as np
import ml_dtypes


def mxq(x, axis, fmt="e4m3"):
    dtype, down = {"e4m3": (ml_dtypes.float8_e4m3fn, 7), "e5m2": (ml_dtypes.float8_e5m2, 14)}[fmt]
    v = np.moveaxis(np.asarray(x, np.float32).astype(ml_dtypes.bfloat16).astype(np.float64), axis, -1)
    blocks = v.reshape(v.shape[:-1] + (-1, 32))
    amax = np.abs(blocks).max(-1, keepdims=True)
    byte = np.maximum(np.where(amax > 0, np.frexp(amax)[1] - 1 + 127, 0) - down, 1)
    scale = np.exp2(byte - 127.0)
    codes = (blocks / scale).astype(np.float32).astype(dtype).astype(np.float64)
    return np.moveaxis((codes * scale).reshape(v.shape), -1, axis)


WIDE = False


def mx_kscale(k):
    if not WIDE:
        return np.ones(k)
    levels = np.array([10, -10, 5, -5, 0])
    if k % 512:
        return np.exp2(np.random.permutation(np.resize(levels, k // 32))).repeat(32)
    a = np.empty((k // 512, 16))
    for p in range(k // 512):
        a[p, :8] = np.random.permutation(np.resize(levels, 8))
        for g in range(8):
            far = levels[np.abs(levels - a[p, g]) >= 10]
            a[p, g + 8] = far[np.random.randint(len(far))]
    return np.exp2(a.ravel()).repeat(32)


def f64(x):
    return np.asarray(x).astype(np.float64)


def striped(idx):
    return np.tile(idx.reshape(-1, 16).T, (8, 1)).astype(np.uint16)


def unstriped(offs):
    return offs[:16].T.reshape(-1).astype(np.int64)


def striped8(idx):
    return np.concatenate([x.reshape(-1, 16).T for x in idx]).astype(np.uint16)


def runs(offs, k):
    lists = np.stack([offs[16 * r : 16 * r + 16].T.reshape(-1) for r in range(8)]).astype(np.int64)
    return lists[np.arange(k) % 512 // 64]


def pack_weight(w):
    k, n = w.shape
    w = f64(np.asarray(w, np.float32).astype(ml_dtypes.bfloat16)).reshape(k // 32, 32, n)
    amax = np.abs(w).max(1)
    byte = np.clip(np.where(amax > 0, np.frexp(amax)[1] - 1 + 127 - 7, 1), 1, 254)
    scaled = (w * np.exp2(127.0 - byte)[:, None, :]).reshape(k, n).astype(np.float32)
    words = np.ascontiguousarray(scaled.reshape(k // 512, 128, 4, n).transpose(0, 1, 3, 2)).astype(ml_dtypes.float8_e4m3fn).view(np.uint8)
    return words, np.ascontiguousarray(byte.astype(np.uint8).reshape(k // 512, 16, n))


def unpack_weight(words, scales):
    g, p, n, _ = words.shape
    vals = np.ascontiguousarray(words).view(ml_dtypes.float8_e4m3fn).astype(np.float64) * np.repeat(np.exp2(scales.astype(np.float64) - 127.0), 8, axis=1)[..., None]
    return vals.transpose(0, 1, 3, 2).reshape(g * 512, n)

def planes(y):
    n, m = y.shape
    v = y.astype(np.float32).astype(ml_dtypes.bfloat16).astype(np.float64).reshape(n // 32, 32, m)
    top = np.abs(v).max(1)
    byte = np.clip(np.where(top > 0, np.frexp(top)[1] - 1 + 127 - 7, 1), 1, 254)
    codes = (v * np.exp2(127.0 - byte)[:, None, :]).reshape(n, m).astype(np.float32).astype(ml_dtypes.float8_e4m3fn).view(np.uint8)
    words = codes.reshape(n // 512, 128, 4, m).transpose(0, 1, 3, 2)
    return np.ascontiguousarray(words), np.ascontiguousarray(byte.astype(np.uint8).reshape(n // 512, 16, m))


K, T, S, G, H, C, W = 512, 1024, 512, 2048, 512, 512, 256


def setup_inputs():
    n = np.random.standard_normal
    s = mx_kscale(K)[:, None]
    packed_xT = pack_weight(n((K, T)) * s)
    packed_dT = pack_weight(n((K, G)) / s)
    perm = np.stack([np.random.permutation(S) for _ in range(8)])
    return {
        "x_words": packed_xT[0],
        "x_scales": packed_xT[1],
        "d_words": packed_dT[0],
        "d_scales": packed_dT[1],
        "gs": (np.random.uniform(0.5, 1.5, (K, 1)) / s).astype(np.float32),
        "offs": striped(np.random.permutation(T)[:S]),
        "k1": striped8(np.random.randint(0, G, (8, H))),
        "n1": striped8(np.stack([np.random.permutation(S) for _ in range(8)])),
        "n2": striped8(np.stack([np.random.permutation(S) for _ in range(8)])),
        "cand": striped(np.random.permutation(T)[:C]),
        "n3": striped8(perm[:, :W]),
        "n4": striped8(perm[:, W:]),
    }


def reference(x_words, x_scales, d_words, d_scales, gs, offs, k1, n1, n2, cand, n3, n4):
    x_cand = unpack_weight(x_words, x_scales)[:, unstriped(cand)]
    d_k1 = unpack_weight(d_words, d_scales)[np.arange(K)[:, None], runs(k1, K)]
    xq = unpack_weight(x_words, x_scales)[:, unstriped(offs)]
    h = 0.0625 * (d_k1.T @ xq)
    st = h + h[np.arange(H)[:, None], runs(n1, H)]
    z = f64(gs) * (st * (np.tanh(st[np.arange(H)[:, None], runs(n2, H)])))
    s = 0.0625 * ((x_cand.T @ mxq(z, 0, "e4m3")))
    pa = s[np.arange(C)[:, None], runs(n3, C)]
    pb = s[np.arange(C)[:, None], runs(n4, C)]
    ra = np.maximum(pa, pb)
    out = s.copy()
    out[np.arange(C)[:, None], runs(n3, C)] = ra
    return (out,) + planes(out)

@@ -1,0 +1,184 @@
+from contextlib import ExitStack
+
+import concourse.mybir as mybir
+
+F32 = mybir.dt.float32
+BF16 = mybir.dt.bfloat16
+I32 = mybir.dt.int32
+U32 = mybir.dt.uint32
+U16 = mybir.dt.uint16
+U8 = mybir.dt.uint8
+FP8X4 = mybir.dt.float8_e4m3fn_x4
+ALU = mybir.AluOpType
+ACT = mybir.ActivationFunctionType
+
+P = 128
+PACK = 4
+N = 512
+HALF = 256
+T = 1024
+G = 2048
+FLOPS = 2 * 2 * 512 * 512 * 512
+
+
+def tile_picked_pqchoppfill_none_po_kernel(
+    tc, x_words, x_scales, d_words, d_scales, gs, offs, k1, n1, n2, cand, n3, n4, out_0, out_1, out_2
+):
+    nc = tc.nc
+    with ExitStack() as ctx:
+        keep = ctx.enter_context(tc.tile_pool(name="keep", bufs=1))
+        psum = ctx.enter_context(tc.psum_pool(name="psum", bufs=1))
+
+        def new(name, shape, dtype, tag=None):
+            return keep.tile(shape, dtype, name=name, tag=tag or name, align_bytes=64)
+
+        def load_list(name, src):
+            tile = new(name, list(src.shape), U16)
+            nc.sync.dma_start(tile[:], src)
+            return tile
+
+        def as_words(src):
+            return src.rearrange("p n t -> p (n t)").bitcast(I32)
+
+        d_bytes = new("d_bytes", [P, G], U8)
+        x_bytes = new("x_bytes", [P, T], U8)
+        w_plane = new("w_plane", [P, N], U8)
+        nc.gpsimd.memset(d_bytes[:].bitcast(I32), 0)
+        nc.vector.memset(x_bytes[:].bitcast(I32), 0)
+        nc.vector.memset(w_plane[:].bitcast(I32), 0)
+
+        offs_list = load_list("offs_list", offs)
+        x_table = new("x_table", [P, T], I32)
+        nc.sync.dma_start(x_table[:], as_words(x_words[0]))
+        k1_list = load_list("k1_list", k1)
+        for e in range(2):
+            nc.sync.dma_start(d_bytes[e:P:16, :].bitcast(I32), d_scales[0, e:16:2, :].bitcast(I32))
+        for q in range(4):
+            nc.sync.dma_start(x_bytes[32 * q : 32 * q + 4, :].bitcast(I32), x_scales[0, 4 * q : 4 * q + 4, :].bitcast(I32))
+        d_table = new("d_table", [P, G], I32)
+        nc.sync.dma_start(d_table[:], as_words(d_words[0]))
+        gain = new("gain", [P, PACK], F32)
+        nc.sync.dma_start(gain[:], gs.rearrange("(p t) o -> p (t o)", t=PACK))
+        cand_list = load_list("cand_list", cand)
+        n1_list = load_list("n1_list", n1)
+        n2_list = load_list("n2_list", n2)
+        n3_list = load_list("n3_list", n3)
+        n4_list = load_list("n4_list", n4)
+
+        warm = new("warm", [P, PACK], F32)
+        nc.scalar.activation(warm[:], gain[:], ACT.Tanh)
+
+        def pick(name, window, offsets, dtype, tag=None):
+            picked = new(name, [P, N], dtype, tag)
+            nc.vector.tensor_copy(picked[:], window.indirect(offsets[:]))
+            return picked
+
+        def deal(name, picked, dtype):
+            dealt = new(name, [P, N], dtype)
+            view = I32 if dtype == U32 else dtype
+            nc.vector.tensor_copy(
+                dealt[:].bitcast(view).rearrange("p (t m) -> p t m", t=PACK),
+                picked[:].bitcast(view).rearrange("p (m t) -> p t m", t=PACK),
+            )
+            return dealt
+
+        tok_words = pick("tok_words", x_table[:].bitcast(U32), offs_list, U32)
+        w_bytes = deal("w_bytes", pick("w_bytes_picked", d_bytes[:], k1_list, U8), U8)
+        for c in range(4):
+            row = 16 * (c // 2) + c % 2
+            nc.sync.dma_start(w_plane[c:P:32, :].bitcast(I32), w_bytes[row:P:32, :].bitcast(I32))
+        tok_plane = pick("tok_plane", x_bytes[:], offs_list, U8)
+        w_words = deal("w_words", pick("w_words_picked", d_table[:].bitcast(U32), k1_list, U32, "picked_words"), U32)
+
+        h_window, h_plain = [], []
+        for t in range(PACK):
+            bank = psum.tile([P, N], F32, name=f"h_bank{t}")
+            cols = slice(t * P, (t + 1) * P)
+            nc.tensor.matmul_mx(
+                out=bank[:], lhsT=w_words[:, cols].bitcast(FP8X4), lhsT_scale=w_plane[:, cols],
+                rhs=tok_words[:].bitcast(FP8X4), rhs_scale=tok_plane[:], start=True, stop=True,
+            )
+            h_window.append(new(f"h_window{t}", [P, N], F32))
+            h_plain.append(new(f"h_plain{t}", [P, N], F32))
+            nc.scalar.activation(h_window[t][:], bank[:], ACT.Copy, scale=0.0625)
+            nc.scalar.activation(h_plain[t][:], bank[:], ACT.Copy, scale=0.0625)
+
+        cand_words = deal("cand_words", pick("cand_words_picked", x_table[:].bitcast(U32), cand_list, U32, "picked_words"), U32)
+
+        def half_cols(u):
+            return slice(u * HALF, (u + 1) * HALF)
+
+        def half_list(offsets, u):
+            return offsets[:, u * 16 : (u + 1) * 16]
+
+        tanh_st, gained = [], []
+        for t in range(PACK):
+            st = new(f"st{t}", [P, N], F32)
+            for u in range(2):
+                nc.vector.tensor_tensor(
+                    st[:, half_cols(u)], h_window[t][:].indirect(half_list(n1_list, u)), h_plain[t][:, half_cols(u)], ALU.add
+                )
+            tanh_st.append(new(f"tanh_st{t}", [P, N], F32))
+            gained.append(new(f"gained{t}", [P, N], F32))
+            nc.scalar.activation(tanh_st[t][:], st[:], ACT.Tanh)
+            nc.scalar.activation(gained[t][:], st[:], ACT.Copy, scale=gain[:, t : t + 1])
+
+        z_rows = []
+        for u in range(2):
+            z = new(f"z{u}", [P, PACK, HALF], F32)
+            for t in range(PACK):
+                nc.vector.tensor_tensor(
+                    z[:, t, :], tanh_st[t][:].indirect(half_list(n2_list, u)), gained[t][:, half_cols(u)], ALU.mult
+                )
+            z_rows.append(new(f"z_rows{u}", [P, HALF, PACK], BF16))
+            nc.scalar.copy(
+                z_rows[u][:].rearrange("p (c i) t -> p c t i", i=4), z[:].rearrange("p t (c i) -> p c t i", i=4)
+            )
+
+        cand_plane = deal("cand_plane", pick("cand_plane_picked", x_bytes[:], cand_list, U8, "tanh_st3"), U8)
+
+        s_banks = [psum.tile([P, N], F32, name=f"s_bank{t}") for t in range(PACK)]
+        scores = [new(f"scores{t}", [P, N], F32) for t in range(PACK)]
+        for u in range(2):
+            z_words = new(f"z_words{u}", [P, HALF], U32)
+            z_plane = new(f"z_plane{u}", [P, HALF], U8)
+            nc.vector.quantize_mx(
+                out=z_words[:].bitcast(FP8X4), scales=z_plane[:], in_=z_rows[u][:].rearrange("p c t -> p (c t)")
+            )
+            for t in range(PACK):
+                cols = slice(t * P, (t + 1) * P)
+                nc.tensor.matmul_mx(
+                    out=s_banks[t][:, half_cols(u)], lhsT=cand_words[:, cols].bitcast(FP8X4), lhsT_scale=cand_plane[:, cols],
+                    rhs=z_words[:].bitcast(FP8X4), rhs_scale=z_plane[:], start=True, stop=True,
+                )
+                nc.scalar.activation(scores[t][:, half_cols(u)], s_banks[t][:, half_cols(u)], ACT.Copy, scale=0.0625)
+
+        out_rows = new("out_rows", [P, N, PACK], BF16)
+        out_dealt = out_0.rearrange("(p t) j -> p t j", t=PACK)
+        for t in range(PACK):
+            pa = new(f"pa{t}", [P, HALF], F32)
+            pb = new(f"pb{t}", [P, HALF], F32)
+            ra = new(f"ra{t}", [P, HALF], F32)
+            nc.vector.tensor_copy(pa[:], scores[t][:].indirect(n3_list[:]))
+            nc.vector.tensor_copy(pb[:], scores[t][:].indirect(n4_list[:]))
+            nc.vector.tensor_tensor(ra[:], pa[:], pb[:], ALU.max)
+            nc.vector.tensor_copy(scores[t][:].indirect(n3_list[:]), ra[:])
+            nc.sync.dma_start(out_dealt[:, t, :], scores[t][:])
+            if t < PACK - 2:
+                nc.scalar.copy(out_rows[:, :, t], scores[t][:])
+            elif t == PACK - 2:
+                nc.scalar.copy(out_rows[:, :, t:], scores[t][:].unsqueeze(2).to_broadcast([P, N, 2]))
+
+        out_words = new("out_words", [P, N], I32)
+        out_plane = new("out_plane", [P, N], U8)
+        for u in range(2):
+            nc.vector.tensor_copy(out_rows[:, half_cols(u), PACK - 1], scores[PACK - 1][:, half_cols(u)])
+        for u in range(2):
+            nc.vector.quantize_mx(
+                out=out_words[:, half_cols(u)].bitcast(FP8X4),
+                scales=out_plane[:, half_cols(u)],
+                in_=out_rows[:, half_cols(u), :].rearrange("p c t -> p (c t)"),
+            )
+            nc.sync.dma_start(as_words(out_1[0])[:, half_cols(u)], out_words[:, half_cols(u)])
+        for q in range(4):
+            nc.scalar.dma_start(out_2[0, 4 * q : 4 * q + 4, :].bitcast(I32), out_plane[32 * q : 32 * q + 4, :].bitcast(I32))

@@ -40,27 +40,36 @@ def tile_picked_pqchoppfill_none_po_kernel(
         def as_words(src):
             return src.rearrange("p n t -> p (n t)").bitcast(I32)
 
+        def half_cols(u):
+            return slice(u * HALF, (u + 1) * HALF)
+
+        def half_list(offsets, u):
+            return offsets[:, u * 16 : (u + 1) * 16]
+
         d_bytes = new("d_bytes", [P, G], U8)
         x_bytes = new("x_bytes", [P, T], U8)
         w_plane = new("w_plane", [P, N], U8)
-        nc.gpsimd.memset(d_bytes[:].bitcast(I32), 0)
-        nc.vector.memset(x_bytes[:].bitcast(I32), 0)
+        h_tiles = [new(f"h_tile{t}", [P, 2 * N], F32) for t in range(PACK)]
+        h_last = new("h_last", [P, N], F32)
+        nc.vector.memset(d_bytes[:].bitcast(I32), 0)
+        nc.gpsimd.memset(x_bytes[:].bitcast(I32), 0)
         nc.vector.memset(w_plane[:].bitcast(I32), 0)
+        nc.vector.memset(h_tiles[0][:, N:], 0.0)
 
-        offs_list = load_list("offs_list", offs)
         x_table = new("x_table", [P, T], I32)
-        nc.sync.dma_start(x_table[:], as_words(x_words[0]))
-        k1_list = load_list("k1_list", k1)
-        for e in range(2):
-            nc.sync.dma_start(d_bytes[e:P:16, :].bitcast(I32), d_scales[0, e:16:2, :].bitcast(I32))
-        for q in range(4):
-            nc.sync.dma_start(x_bytes[32 * q : 32 * q + 4, :].bitcast(I32), x_scales[0, 4 * q : 4 * q + 4, :].bitcast(I32))
         d_table = new("d_table", [P, G], I32)
-        nc.sync.dma_start(d_table[:], as_words(d_words[0]))
         gain = new("gain", [P, PACK], F32)
-        nc.sync.dma_start(gain[:], gs.rearrange("(p t) o -> p (t o)", t=PACK))
+        k1_list = load_list("k1_list", k1)
+        offs_list = load_list("offs_list", offs)
         cand_list = load_list("cand_list", cand)
         n1_list = load_list("n1_list", n1)
+        for e in range(2):
+            nc.sync.dma_start(d_bytes[e:P:16, :].bitcast(I32), d_scales[0, e:16:2, :].bitcast(I32))
+        nc.sync.dma_start(x_table[:], as_words(x_words[0]))
+        for q in range(4):
+            nc.sync.dma_start(x_bytes[32 * q : 32 * q + 4, :].bitcast(I32), x_scales[0, 4 * q : 4 * q + 4, :].bitcast(I32))
+        nc.sync.dma_start(gain[:], gs.rearrange("(p t) o -> p (t o)", t=PACK))
+        nc.sync.dma_start(d_table[:], as_words(d_words[0]))
         n2_list = load_list("n2_list", n2)
         n3_list = load_list("n3_list", n3)
         n4_list = load_list("n4_list", n4)
@@ -75,22 +84,27 @@ def tile_picked_pqchoppfill_none_po_kernel(
 
         def deal(name, picked, dtype):
             dealt = new(name, [P, N], dtype)
-            view = I32 if dtype == U32 else dtype
             nc.vector.tensor_copy(
-                dealt[:].bitcast(view).rearrange("p (t m) -> p t m", t=PACK),
-                picked[:].bitcast(view).rearrange("p (m t) -> p t m", t=PACK),
+                dealt[:].rearrange("p (t m i) -> p m t i", t=PACK, i=4),
+                picked[:].rearrange("p (m i t) -> p m t i", t=PACK, i=4),
             )
             return dealt
 
-        tok_words = pick("tok_words", x_table[:].bitcast(U32), offs_list, U32)
         w_bytes = deal("w_bytes", pick("w_bytes_picked", d_bytes[:], k1_list, U8), U8)
         for c in range(4):
             row = 16 * (c // 2) + c % 2
             nc.sync.dma_start(w_plane[c:P:32, :].bitcast(I32), w_bytes[row:P:32, :].bitcast(I32))
+        tok_words = pick("tok_words", x_table[:].bitcast(U32), offs_list, U32)
         tok_plane = pick("tok_plane", x_bytes[:], offs_list, U8)
-        w_words = deal("w_words", pick("w_words_picked", d_table[:].bitcast(U32), k1_list, U32, "picked_words"), U32)
+        w_picked = pick("w_words_picked", d_table[:].bitcast(U32), k1_list, U32, "picked_words")
+        w_words = new("w_words", [P, N], U32)
+        for slots in (slice(0, 1), slice(1, PACK)):
+            nc.vector.tensor_copy(
+                w_words[:].rearrange("p (t m i) -> p m t i", t=PACK, i=4)[:, :, slots, :],
+                w_picked[:].rearrange("p (m i t) -> p m t i", t=PACK, i=4)[:, :, slots, :],
+            )
 
-        h_window, h_plain = [], []
+        h_plain = [h_tiles[t + 1][:, N:] for t in range(PACK - 1)] + [h_last[:]]
         for t in range(PACK):
             bank = psum.tile([P, N], F32, name=f"h_bank{t}")
             cols = slice(t * P, (t + 1) * P)
@@ -98,81 +112,112 @@ def tile_picked_pqchoppfill_none_po_kernel(
                 out=bank[:], lhsT=w_words[:, cols].bitcast(FP8X4), lhsT_scale=w_plane[:, cols],
                 rhs=tok_words[:].bitcast(FP8X4), rhs_scale=tok_plane[:], start=True, stop=True,
             )
-            h_window.append(new(f"h_window{t}", [P, N], F32))
-            h_plain.append(new(f"h_plain{t}", [P, N], F32))
-            nc.scalar.activation(h_window[t][:], bank[:], ACT.Copy, scale=0.0625)
-            nc.scalar.activation(h_plain[t][:], bank[:], ACT.Copy, scale=0.0625)
+            nc.scalar.activation(h_tiles[t][:, :N], bank[:], ACT.Copy, scale=0.0625)
+            nc.scalar.activation(h_plain[t], bank[:], ACT.Copy, scale=0.0625)
 
         cand_words = deal("cand_words", pick("cand_words_picked", x_table[:].bitcast(U32), cand_list, U32, "picked_words"), U32)
 
-        def half_cols(u):
-            return slice(u * HALF, (u + 1) * HALF)
+        states, tanh_st, gained = [], [], []
 
-        def half_list(offsets, u):
-            return offsets[:, u * 16 : (u + 1) * 16]
+        def gain_cols(t, cols):
+            nc.scalar.activation(gained[t][:, cols], states[t][:, cols], ACT.Copy, scale=gain[:, t : t + 1])
 
-        tanh_st, gained = [], []
+        early = 1
         for t in range(PACK):
-            st = new(f"st{t}", [P, N], F32)
-            for u in range(2):
-                nc.vector.tensor_tensor(
-                    st[:, half_cols(u)], h_window[t][:].indirect(half_list(n1_list, u)), h_plain[t][:, half_cols(u)], ALU.add
-                )
+            states.append(new(f"st{t}", [P, N], F32))
+            nc.vector.tensor_tensor(states[t][:], h_tiles[t][:].indirect(n1_list[:]), h_plain[t], ALU.add)
             tanh_st.append(new(f"tanh_st{t}", [P, N], F32))
             gained.append(new(f"gained{t}", [P, N], F32))
-            nc.scalar.activation(tanh_st[t][:], st[:], ACT.Tanh)
-            nc.scalar.activation(gained[t][:], st[:], ACT.Copy, scale=gain[:, t : t + 1])
+            nc.scalar.activation(tanh_st[t][:], states[t][:], ACT.Tanh)
+            gain_cols(t, slice(0, N) if t < early else half_cols(0))
+        for t in range(early, PACK):
+            gain_cols(t, half_cols(1))
 
-        z_rows = []
+        z = [new(f"z{u}", [P, PACK, HALF], F32) for u in range(2)]
+        z_rows = [new(f"z_rows{u}", [P, HALF, PACK], BF16) for u in range(2)]
+
+        def make_z(u, t):
+            nc.vector.tensor_tensor(
+                z[u][:, t, :], tanh_st[t][:].indirect(half_list(n2_list, u)), gained[t][:, half_cols(u)], ALU.mult
+            )
+
+        for t in range(early):
+            make_z(0, t)
+            make_z(1, t)
         for u in range(2):
-            z = new(f"z{u}", [P, PACK, HALF], F32)
-            for t in range(PACK):
-                nc.vector.tensor_tensor(
-                    z[:, t, :], tanh_st[t][:].indirect(half_list(n2_list, u)), gained[t][:, half_cols(u)], ALU.mult
-                )
-            z_rows.append(new(f"z_rows{u}", [P, HALF, PACK], BF16))
+            for t in range(early, PACK):
+                make_z(u, t)
             nc.scalar.copy(
-                z_rows[u][:].rearrange("p (c i) t -> p c t i", i=4), z[:].rearrange("p t (c i) -> p c t i", i=4)
+                z_rows[u][:].rearrange("p (c i) t -> p c t i", i=4), z[u][:].rearrange("p t (c i) -> p c t i", i=4)
             )
 
         cand_plane = deal("cand_plane", pick("cand_plane_picked", x_bytes[:], cand_list, U8, "tanh_st3"), U8)
 
+        order = [2, 0, 1, 3]
         s_banks = [psum.tile([P, N], F32, name=f"s_bank{t}") for t in range(PACK)]
         scores = [new(f"scores{t}", [P, N], F32) for t in range(PACK)]
-        for u in range(2):
-            z_words = new(f"z_words{u}", [P, HALF], U32)
-            z_plane = new(f"z_plane{u}", [P, HALF], U8)
-            nc.vector.quantize_mx(
-                out=z_words[:].bitcast(FP8X4), scales=z_plane[:], in_=z_rows[u][:].rearrange("p c t -> p (c t)")
+        z_words = new("z_words", [P, N], U32)
+        z_plane = new("z_plane", [P, N], U8)
+
+        def score(t, cols):
+            rows = slice(t * P, (t + 1) * P)
+            nc.tensor.matmul_mx(
+                out=s_banks[t][:, cols], lhsT=cand_words[:, rows].bitcast(FP8X4), lhsT_scale=cand_plane[:, rows],
+                rhs=z_words[:, cols].bitcast(FP8X4), rhs_scale=z_plane[:, cols], start=True, stop=True,
             )
-            for t in range(PACK):
-                cols = slice(t * P, (t + 1) * P)
-                nc.tensor.matmul_mx(
-                    out=s_banks[t][:, half_cols(u)], lhsT=cand_words[:, cols].bitcast(FP8X4), lhsT_scale=cand_plane[:, cols],
-                    rhs=z_words[:].bitcast(FP8X4), rhs_scale=z_plane[:], start=True, stop=True,
-                )
-                nc.scalar.activation(scores[t][:, half_cols(u)], s_banks[t][:, half_cols(u)], ACT.Copy, scale=0.0625)
+            nc.scalar.activation(scores[t][:, cols], s_banks[t][:, cols], ACT.Copy, scale=0.0625)
+
+        for u in range(2):
+            nc.vector.quantize_mx(
+                out=z_words[:, half_cols(u)].bitcast(FP8X4),
+                scales=z_plane[:, half_cols(u)],
+                in_=z_rows[u][:].rearrange("p c t -> p (c t)"),
+            )
+            for t in order[:1]:
+                score(t, half_cols(u))
+        for t in order[1:]:
+            score(t, slice(0, N))
 
         out_rows = new("out_rows", [P, N, PACK], BF16)
         out_dealt = out_0.rearrange("(p t) j -> p t j", t=PACK)
-        for t in range(PACK):
-            pa = new(f"pa{t}", [P, HALF], F32)
-            pb = new(f"pb{t}", [P, HALF], F32)
-            ra = new(f"ra{t}", [P, HALF], F32)
-            nc.vector.tensor_copy(pa[:], scores[t][:].indirect(n3_list[:]))
-            nc.vector.tensor_copy(pb[:], scores[t][:].indirect(n4_list[:]))
-            nc.vector.tensor_tensor(ra[:], pa[:], pb[:], ALU.max)
-            nc.vector.tensor_copy(scores[t][:].indirect(n3_list[:]), ra[:])
+        pa, lift = {}, {}
+
+        def fetch(step):
+            t = order[step]
+            pa[t] = new(f"pa{t}", [P, HALF], F32, f"pa_slot{step % 3}")
+            nc.vector.tensor_copy(pa[t][:], scores[t][:].indirect(n3_list[:]))
+
+        def compare(step):
+            t = order[step]
+            gap = new(f"gap{t}", [P, HALF], F32, f"gap{step}" if step < 2 else f"lift{step - 2}")
+            lift[t] = new(f"lift{t}", [P, HALF], F32, f"lift{step}")
+            nc.vector.tensor_tensor(gap[:], scores[t][:].indirect(n4_list[:]), pa[t][:], ALU.subtract)
+            nc.scalar.activation(lift[t][:], gap[:], ACT.Relu)
+
+        def put_back(step):
+            t = order[step]
+            nc.vector.tensor_tensor(scores[t][:].indirect(n3_list[:]), pa[t][:], lift[t][:], ALU.add)
             nc.sync.dma_start(out_dealt[:, t, :], scores[t][:])
             if t < PACK - 2:
                 nc.scalar.copy(out_rows[:, :, t], scores[t][:])
             elif t == PACK - 2:
                 nc.scalar.copy(out_rows[:, :, t:], scores[t][:].unsqueeze(2).to_broadcast([P, N, 2]))
 
+        fetch(0)
+        fetch(1)
+        compare(0)
+        compare(1)
+        for step in range(PACK):
+            if step + 2 < PACK:
+                fetch(step + 2)
+            put_back(step)
+            if step + 2 < PACK:
+                compare(step + 2)
+
         out_words = new("out_words", [P, N], I32)
         out_plane = new("out_plane", [P, N], U8)
-        for u in range(2):
-            nc.vector.tensor_copy(out_rows[:, half_cols(u), PACK - 1], scores[PACK - 1][:, half_cols(u)])
+        nc.vector.tensor_copy(out_rows[:, half_cols(0), PACK - 1], scores[PACK - 1][:, half_cols(0)])
+        nc.scalar.copy(out_rows[:, half_cols(1), PACK - 1], scores[PACK - 1][:, half_cols(1)])
         for u in range(2):
             nc.vector.quantize_mx(
                 out=out_words[:, half_cols(u)].bitcast(FP8X4),
@@ -181,4 +226,4 @@ def tile_picked_pqchoppfill_none_po_kernel(
             )
             nc.sync.dma_start(as_words(out_1[0])[:, half_cols(u)], out_words[:, half_cols(u)])
         for q in range(4):
-            nc.scalar.dma_start(out_2[0, 4 * q : 4 * q + 4, :].bitcast(I32), out_plane[32 * q : 32 * q + 4, :].bitcast(I32))
+            (nc.sync if q == 0 else nc.scalar).dma_start(out_2[0, 4 * q : 4 * q + 4, :].bitcast(I32), out_plane[32 * q : 32 * q + 4, :].bitcast(I32))

@@ -50,11 +50,12 @@ def tile_picked_pqchoppfill_none_po_kernel(
         x_bytes = new("x_bytes", [P, T], U8)
         w_plane = new("w_plane", [P, N], U8)
         h_tiles = [new(f"h_tile{t}", [P, 2 * N], F32) for t in range(PACK)]
-        h_last = new("h_last", [P, N], F32)
-        nc.vector.memset(d_bytes[:].bitcast(I32), 0)
-        nc.gpsimd.memset(x_bytes[:].bitcast(I32), 0)
+        nc.vector.memset(d_bytes[:, : G // 2].bitcast(I32), 0)
+        nc.gpsimd.memset(d_bytes[:, G // 2 :].bitcast(I32), 0)
+        nc.vector.memset(x_bytes[:].bitcast(I32), 0)
         nc.vector.memset(w_plane[:].bitcast(I32), 0)
-        nc.vector.memset(h_tiles[0][:, N:], 0.0)
+        for tile in h_tiles[:2]:
+            nc.vector.memset(tile[:, N:].bitcast(I32), 0)
 
         x_table = new("x_table", [P, T], I32)
         d_table = new("d_table", [P, G], I32)
@@ -104,16 +105,27 @@ def tile_picked_pqchoppfill_none_po_kernel(
                 w_picked[:].rearrange("p (m i t) -> p m t i", t=PACK, i=4)[:, :, slots, :],
             )
 
-        h_plain = [h_tiles[t + 1][:, N:] for t in range(PACK - 1)] + [h_last[:]]
-        for t in range(PACK):
-            bank = psum.tile([P, N], F32, name=f"h_bank{t}")
-            cols = slice(t * P, (t + 1) * P)
+        h_plain = [new("h_plain0", [P, N], F32)[:], h_tiles[2][:, N:], h_tiles[3][:, N:], new("h_plain3", [P, N], F32)[:]]
+        def layer(t, cols, bank):
+            rows = slice(t * P, (t + 1) * P)
             nc.tensor.matmul_mx(
-                out=bank[:], lhsT=w_words[:, cols].bitcast(FP8X4), lhsT_scale=w_plane[:, cols],
-                rhs=tok_words[:].bitcast(FP8X4), rhs_scale=tok_plane[:], start=True, stop=True,
+                out=bank[:, cols], lhsT=w_words[:, rows].bitcast(FP8X4), lhsT_scale=w_plane[:, rows],
+                rhs=tok_words[:, cols].bitcast(FP8X4), rhs_scale=tok_plane[:, cols], start=True, stop=True,
             )
-            nc.scalar.activation(h_tiles[t][:, :N], bank[:], ACT.Copy, scale=0.0625)
-            nc.scalar.activation(h_plain[t], bank[:], ACT.Copy, scale=0.0625)
+            nc.scalar.activation(h_tiles[t][:, cols], bank[:, cols], ACT.Copy, scale=0.0625)
+
+        def plain(t, cols, bank):
+            nc.scalar.activation(h_plain[t][:, cols], bank[:, cols], ACT.Copy, scale=0.0625)
+
+        half_banks = [psum.tile([P, N], F32, name=f"h_half{u}", tag=f"s_bank{u + 2}") for u in range(2)]
+        for u in range(2):
+            layer(0, half_cols(u), half_banks[u])
+        for u in range(2):
+            plain(0, half_cols(u), half_banks[u])
+        for t in range(1, PACK):
+            bank = psum.tile([P, N], F32, name=f"h_bank{t}")
+            layer(t, slice(0, N), bank)
+            plain(t, slice(0, N), bank)
 
         cand_words = deal("cand_words", pick("cand_words_picked", x_table[:].bitcast(U32), cand_list, U32, "picked_words"), U32)
 
@@ -151,21 +163,24 @@ def tile_picked_pqchoppfill_none_po_kernel(
                 z_rows[u][:].rearrange("p (c i) t -> p c t i", i=4), z[u][:].rearrange("p t (c i) -> p c t i", i=4)
             )
 
-        cand_plane = deal("cand_plane", pick("cand_plane_picked", x_bytes[:], cand_list, U8, "tanh_st3"), U8)
+        cand_picked = pick("cand_plane_picked", x_bytes[:], cand_list, U8, "tanh_st3")
+        by_slot = cand_picked[:].rearrange("p (m i t) -> p m t i", t=PACK, i=4)
+        first_plane = new("first_plane", [P, P], U8)
+        nc.vector.tensor_copy(first_plane[:].rearrange("p (m i) -> p m i", i=4), by_slot[:, :, 0, :])
 
-        order = [2, 0, 1, 3]
+        order = [0, 2, 1, 3]
         s_banks = [psum.tile([P, N], F32, name=f"s_bank{t}") for t in range(PACK)]
         scores = [new(f"scores{t}", [P, N], F32) for t in range(PACK)]
         z_words = new("z_words", [P, N], U32)
         z_plane = new("z_plane", [P, N], U8)
 
-        def score(t, cols):
+        def score(t, cols, bank, plane):
             rows = slice(t * P, (t + 1) * P)
             nc.tensor.matmul_mx(
-                out=s_banks[t][:, cols], lhsT=cand_words[:, rows].bitcast(FP8X4), lhsT_scale=cand_plane[:, rows],
+                out=bank[:, cols], lhsT=cand_words[:, rows].bitcast(FP8X4), lhsT_scale=plane,
                 rhs=z_words[:, cols].bitcast(FP8X4), rhs_scale=z_plane[:, cols], start=True, stop=True,
             )
-            nc.scalar.activation(scores[t][:, cols], s_banks[t][:, cols], ACT.Copy, scale=0.0625)
+            nc.scalar.activation(scores[t][:, cols], bank[:, cols], ACT.Copy, scale=0.0625)
 
         for u in range(2):
             nc.vector.quantize_mx(
@@ -174,9 +189,11 @@ def tile_picked_pqchoppfill_none_po_kernel(
                 in_=z_rows[u][:].rearrange("p c t -> p (c t)"),
             )
             for t in order[:1]:
-                score(t, half_cols(u))
+                score(t, half_cols(u), s_banks[t] if u else psum.tile([P, N], F32, name=f"first_half{t}", tag=f"h_bank{t}"), first_plane[:])
+        rest_plane = new("rest_plane", [P, (PACK - 1) * P], U8, "z_rows1")
+        nc.vector.tensor_copy(rest_plane[:].rearrange("p (t m i) -> p m t i", t=PACK - 1, i=4), by_slot[:, :, 1:, :])
         for t in order[1:]:
-            score(t, slice(0, N))
+            score(t, slice(0, N), s_banks[t], rest_plane[:, (t - 1) * P : t * P])
 
         out_rows = new("out_rows", [P, N, PACK], BF16)
         out_dealt = out_0.rearrange("(p t) j -> p t j", t=PACK)
@@ -216,8 +233,10 @@ def tile_picked_pqchoppfill_none_po_kernel(
 
         out_words = new("out_words", [P, N], I32)
         out_plane = new("out_plane", [P, N], U8)
-        nc.vector.tensor_copy(out_rows[:, half_cols(0), PACK - 1], scores[PACK - 1][:, half_cols(0)])
-        nc.scalar.copy(out_rows[:, half_cols(1), PACK - 1], scores[PACK - 1][:, half_cols(1)])
+        cut = 384
+        for cols in (slice(0, HALF), slice(HALF, cut)):
+            nc.vector.tensor_copy(out_rows[:, cols, PACK - 1], scores[PACK - 1][:, cols])
+        nc.scalar.copy(out_rows[:, cut:, PACK - 1], scores[PACK - 1][:, cut:])
         for u in range(2):
             nc.vector.quantize_mx(
                 out=out_words[:, half_cols(u)].bitcast(FP8X4),

@@ -13,12 +13,20 @@ ALU = mybir.AluOpType
 ACT = mybir.ActivationFunctionType
 
 P = 128
-PACK = 4
+SLOTS = 4
 N = 512
-HALF = 256
-T = 1024
-G = 2048
-FLOPS = 2 * 2 * 512 * 512 * 512
+HALF = N // 2
+TOKENS = 1024
+CODEWORDS = 2048
+GROUP = 16
+QUADRANT = 32
+PLANE_ROWS = 4
+LINE = 4
+SIXTEENTH = 0.0625
+SCORE_ORDER = (0, 2, 1, 3)
+PA_BUFFERS = 3
+VECTOR_COLUMNS = 384
+FLOPS = 2 * 2 * N * N * N
 
 
 def tile_picked_pqchoppfill_none_po_kernel(
@@ -32,217 +40,237 @@ def tile_picked_pqchoppfill_none_po_kernel(
         def new(name, shape, dtype, tag=None):
             return keep.tile(shape, dtype, name=name, tag=tag or name, align_bytes=64)
 
+        def new_bank(name, tag=None):
+            return psum.tile([P, N], F32, name=name, tag=tag or name)
+
         def load_list(name, src):
             tile = new(name, list(src.shape), U16)
             nc.sync.dma_start(tile[:], src)
             return tile
 
-        def as_words(src):
-            return src.rearrange("p n t -> p (n t)").bitcast(I32)
+        def as_words(codes):
+            return codes.rearrange("p n t -> p (n t)").bitcast(I32)
 
         def half_cols(u):
             return slice(u * HALF, (u + 1) * HALF)
 
         def half_list(offsets, u):
-            return offsets[:, u * 16 : (u + 1) * 16]
+            return offsets[:, u * HALF // GROUP : (u + 1) * HALF // GROUP]
 
-        d_bytes = new("d_bytes", [P, G], U8)
-        x_bytes = new("x_bytes", [P, T], U8)
+        def in_list_order(picked):
+            return picked.rearrange("p (m i t) -> p m t i", t=SLOTS, i=LINE)
+
+        def in_slot_order(dealt, slots):
+            return dealt.rearrange("p (t m i) -> p m t i", t=slots, i=LINE)
+
+        d_bytes = new("d_bytes", [P, CODEWORDS], U8)
+        x_bytes = new("x_bytes", [P, TOKENS], U8)
         w_plane = new("w_plane", [P, N], U8)
-        h_tiles = [new(f"h_tile{t}", [P, 2 * N], F32) for t in range(PACK)]
-        nc.vector.memset(d_bytes[:, : G // 2].bitcast(I32), 0)
-        nc.gpsimd.memset(d_bytes[:, G // 2 :].bitcast(I32), 0)
+        nc.vector.memset(d_bytes[:, : CODEWORDS // 2].bitcast(I32), 0)
+        nc.gpsimd.memset(d_bytes[:, CODEWORDS // 2 :].bitcast(I32), 0)
         nc.vector.memset(x_bytes[:].bitcast(I32), 0)
         nc.vector.memset(w_plane[:].bitcast(I32), 0)
-        for tile in h_tiles[:2]:
-            nc.vector.memset(tile[:, N:].bitcast(I32), 0)
 
-        x_table = new("x_table", [P, T], I32)
-        d_table = new("d_table", [P, G], I32)
-        gain = new("gain", [P, PACK], F32)
+        h_windows = [new(f"h_window{t}", [P, 2 * N], F32) for t in range(SLOTS)]
+        for window in h_windows[:2]:
+            nc.vector.memset(window[:, N:].bitcast(I32), 0)
+
+        x_table = new("x_table", [P, TOKENS], I32)
+        d_table = new("d_table", [P, CODEWORDS], I32)
+        gain = new("gain", [P, SLOTS], F32)
         k1_list = load_list("k1_list", k1)
         offs_list = load_list("offs_list", offs)
         cand_list = load_list("cand_list", cand)
         n1_list = load_list("n1_list", n1)
         for e in range(2):
-            nc.sync.dma_start(d_bytes[e:P:16, :].bitcast(I32), d_scales[0, e:16:2, :].bitcast(I32))
+            nc.sync.dma_start(d_bytes[e:P:GROUP, :].bitcast(I32), d_scales[0, e::2, :].bitcast(I32))
         nc.sync.dma_start(x_table[:], as_words(x_words[0]))
-        for q in range(4):
-            nc.sync.dma_start(x_bytes[32 * q : 32 * q + 4, :].bitcast(I32), x_scales[0, 4 * q : 4 * q + 4, :].bitcast(I32))
-        nc.sync.dma_start(gain[:], gs.rearrange("(p t) o -> p (t o)", t=PACK))
         nc.sync.dma_start(d_table[:], as_words(d_words[0]))
+        for q in range(P // QUADRANT):
+            nc.sync.dma_start(
+                x_bytes[QUADRANT * q : QUADRANT * q + PLANE_ROWS, :].bitcast(I32),
+                x_scales[0, PLANE_ROWS * q : PLANE_ROWS * (q + 1), :].bitcast(I32),
+            )
+        nc.sync.dma_start(gain[:], gs.rearrange("(p t) o -> p (t o)", t=SLOTS))
         n2_list = load_list("n2_list", n2)
         n3_list = load_list("n3_list", n3)
         n4_list = load_list("n4_list", n4)
 
-        warm = new("warm", [P, PACK], F32)
+        warm = new("warm", [P, SLOTS], F32)
         nc.scalar.activation(warm[:], gain[:], ACT.Tanh)
 
         def pick(name, window, offsets, dtype, tag=None):
-            picked = new(name, [P, N], dtype, tag)
-            nc.vector.tensor_copy(picked[:], window.indirect(offsets[:]))
+            picked = new(name, [P, GROUP * offsets.shape[1]], dtype, tag)
+            nc.vector.tensor_copy(picked[:], window.indirect(offsets))
             return picked
 
-        def deal(name, picked, dtype):
-            dealt = new(name, [P, N], dtype)
-            nc.vector.tensor_copy(
-                dealt[:].rearrange("p (t m i) -> p m t i", t=PACK, i=4),
-                picked[:].rearrange("p (m i t) -> p m t i", t=PACK, i=4),
-            )
+        def deal(name, picked, slots, dtype, tag=None):
+            count = slots.stop - slots.start
+            dealt = new(name, [P, count * P], dtype, tag)
+            nc.vector.tensor_copy(in_slot_order(dealt[:], count), in_list_order(picked[:])[:, :, slots, :])
             return dealt
 
-        w_bytes = deal("w_bytes", pick("w_bytes_picked", d_bytes[:], k1_list, U8), U8)
-        for c in range(4):
-            row = 16 * (c // 2) + c % 2
-            nc.sync.dma_start(w_plane[c:P:32, :].bitcast(I32), w_bytes[row:P:32, :].bitcast(I32))
-        tok_words = pick("tok_words", x_table[:].bitcast(U32), offs_list, U32)
-        tok_plane = pick("tok_plane", x_bytes[:], offs_list, U8)
-        w_picked = pick("w_words_picked", d_table[:].bitcast(U32), k1_list, U32, "picked_words")
-        w_words = new("w_words", [P, N], U32)
-        for slots in (slice(0, 1), slice(1, PACK)):
-            nc.vector.tensor_copy(
-                w_words[:].rearrange("p (t m i) -> p m t i", t=PACK, i=4)[:, :, slots, :],
-                w_picked[:].rearrange("p (m i t) -> p m t i", t=PACK, i=4)[:, :, slots, :],
-            )
+        every_slot, first_slot, other_slots = slice(0, SLOTS), slice(0, 1), slice(1, SLOTS)
 
-        h_plain = [new("h_plain0", [P, N], F32)[:], h_tiles[2][:, N:], h_tiles[3][:, N:], new("h_plain3", [P, N], F32)[:]]
-        def layer(t, cols, bank):
+        w_bytes = deal("w_bytes", pick("w_bytes_picked", d_bytes[:], k1_list[:], U8), every_slot, U8)
+        for c in range(PLANE_ROWS):
+            row = GROUP * (c // 2) + c % 2
+            nc.sync.dma_start(w_plane[c:P:QUADRANT, :].bitcast(I32), w_bytes[row:P:QUADRANT, :].bitcast(I32))
+        token_words = pick("token_words", x_table[:].bitcast(U32), offs_list[:], U32)
+        w_picked = pick("w_picked", d_table[:].bitcast(U32), k1_list[:], U32)
+        token_planes = [pick("token_plane0", x_bytes[:], half_list(offs_list, 0), U8)]
+        w_words = deal("w_words", w_picked, every_slot, U32)
+        token_planes.append(pick("token_plane1", x_bytes[:], half_list(offs_list, 1), U8))
+
+        h_plain = [new("h_plain0", [P, N], F32)[:], h_windows[2][:, N:], h_windows[3][:, N:], new("h_plain3", [P, N], F32)[:]]
+
+        def layer_product(t, u, bank):
             rows = slice(t * P, (t + 1) * P)
             nc.tensor.matmul_mx(
-                out=bank[:, cols], lhsT=w_words[:, rows].bitcast(FP8X4), lhsT_scale=w_plane[:, rows],
-                rhs=tok_words[:, cols].bitcast(FP8X4), rhs_scale=tok_plane[:, cols], start=True, stop=True,
+                out=bank[:, half_cols(u)],
+                lhsT=w_words[:, rows].bitcast(FP8X4),
+                lhsT_scale=w_plane[:, rows],
+                rhs=token_words[:, half_cols(u)].bitcast(FP8X4),
+                rhs_scale=token_planes[u][:],
+                start=True,
+                stop=True,
             )
-            nc.scalar.activation(h_tiles[t][:, cols], bank[:, cols], ACT.Copy, scale=0.0625)
 
-        def plain(t, cols, bank):
-            nc.scalar.activation(h_plain[t][:, cols], bank[:, cols], ACT.Copy, scale=0.0625)
+        def copy_h(t, cols, bank):
+            nc.scalar.activation(h_windows[t][:, cols], bank[:, cols], ACT.Copy, scale=SIXTEENTH)
+            nc.scalar.activation(h_plain[t][:, cols], bank[:, cols], ACT.Copy, scale=SIXTEENTH)
 
-        half_banks = [psum.tile([P, N], F32, name=f"h_half{u}", tag=f"s_bank{u + 2}") for u in range(2)]
         for u in range(2):
-            layer(0, half_cols(u), half_banks[u])
-        for u in range(2):
-            plain(0, half_cols(u), half_banks[u])
-        for t in range(1, PACK):
-            bank = psum.tile([P, N], F32, name=f"h_bank{t}")
-            layer(t, slice(0, N), bank)
-            plain(t, slice(0, N), bank)
+            bank = new_bank(f"h_half{u}", f"s_bank{u + 2}")
+            layer_product(0, u, bank)
+            copy_h(0, half_cols(u), bank)
+        for t in range(1, SLOTS):
+            bank = new_bank(f"h_bank{t}")
+            for u in range(2):
+                layer_product(t, u, bank)
+            copy_h(t, slice(0, N), bank)
 
-        cand_words = deal("cand_words", pick("cand_words_picked", x_table[:].bitcast(U32), cand_list, U32, "picked_words"), U32)
+        cand_picked = pick("cand_picked", x_table[:].bitcast(U32), cand_list[:], U32, "w_bytes")
+        first_words = deal("first_words", cand_picked, first_slot, U32)
 
-        states, tanh_st, gained = [], [], []
+        states, tanh_windows, gained = [], [], []
 
-        def gain_cols(t, cols):
+        def apply_gain(t, cols):
             nc.scalar.activation(gained[t][:, cols], states[t][:, cols], ACT.Copy, scale=gain[:, t : t + 1])
 
-        early = 1
-        for t in range(PACK):
-            states.append(new(f"st{t}", [P, N], F32))
-            nc.vector.tensor_tensor(states[t][:], h_tiles[t][:].indirect(n1_list[:]), h_plain[t], ALU.add)
-            tanh_st.append(new(f"tanh_st{t}", [P, N], F32))
+        for t in range(SLOTS):
+            states.append(new(f"state{t}", [P, N], F32))
+            nc.vector.tensor_tensor(states[t][:], h_windows[t][:].indirect(n1_list[:]), h_plain[t], ALU.add)
+            tanh_windows.append(new(f"tanh_window{t}", [P, N], F32))
             gained.append(new(f"gained{t}", [P, N], F32))
-            nc.scalar.activation(tanh_st[t][:], states[t][:], ACT.Tanh)
-            gain_cols(t, slice(0, N) if t < early else half_cols(0))
-        for t in range(early, PACK):
-            gain_cols(t, half_cols(1))
+            nc.scalar.activation(tanh_windows[t][:], states[t][:], ACT.Tanh)
+            apply_gain(t, slice(0, N) if t == 0 else half_cols(0))
+        for t in range(1, SLOTS):
+            apply_gain(t, half_cols(1))
 
-        z = [new(f"z{u}", [P, PACK, HALF], F32) for u in range(2)]
-        z_rows = [new(f"z_rows{u}", [P, HALF, PACK], BF16) for u in range(2)]
+        z_halves = [new(f"z_half{u}", [P, SLOTS, HALF], F32) for u in range(2)]
+        z_rounded = [new(f"z_rounded{u}", [P, HALF, SLOTS], BF16) for u in range(2)]
 
         def make_z(u, t):
             nc.vector.tensor_tensor(
-                z[u][:, t, :], tanh_st[t][:].indirect(half_list(n2_list, u)), gained[t][:, half_cols(u)], ALU.mult
+                z_halves[u][:, t, :], tanh_windows[t][:].indirect(half_list(n2_list, u)), gained[t][:, half_cols(u)], ALU.mult
             )
 
-        for t in range(early):
-            make_z(0, t)
-            make_z(1, t)
         for u in range(2):
-            for t in range(early, PACK):
+            make_z(u, 0)
+        for u in range(2):
+            for t in range(1, SLOTS):
                 make_z(u, t)
             nc.scalar.copy(
-                z_rows[u][:].rearrange("p (c i) t -> p c t i", i=4), z[u][:].rearrange("p t (c i) -> p c t i", i=4)
+                z_rounded[u][:].rearrange("p (c i) t -> p c t i", i=LINE),
+                z_halves[u][:].rearrange("p t (c i) -> p c t i", i=LINE),
             )
 
-        cand_picked = pick("cand_plane_picked", x_bytes[:], cand_list, U8, "tanh_st3")
-        by_slot = cand_picked[:].rearrange("p (m i t) -> p m t i", t=PACK, i=4)
-        first_plane = new("first_plane", [P, P], U8)
-        nc.vector.tensor_copy(first_plane[:].rearrange("p (m i) -> p m i", i=4), by_slot[:, :, 0, :])
+        cand_bytes = pick("cand_bytes", x_bytes[:], cand_list[:], U8, f"tanh_window{SLOTS - 1}")
+        first_plane = deal("first_plane", cand_bytes, first_slot, U8)
 
-        order = [0, 2, 1, 3]
-        s_banks = [psum.tile([P, N], F32, name=f"s_bank{t}") for t in range(PACK)]
-        scores = [new(f"scores{t}", [P, N], F32) for t in range(PACK)]
+        s_banks = [new_bank(f"s_bank{t}") for t in range(SLOTS)]
+        scores = [new(f"scores{t}", [P, N], F32) for t in range(SLOTS)]
         z_words = new("z_words", [P, N], U32)
         z_plane = new("z_plane", [P, N], U8)
 
-        def score(t, cols, bank, plane):
-            rows = slice(t * P, (t + 1) * P)
+        def score(t, cols, bank, words, plane):
             nc.tensor.matmul_mx(
-                out=bank[:, cols], lhsT=cand_words[:, rows].bitcast(FP8X4), lhsT_scale=plane,
-                rhs=z_words[:, cols].bitcast(FP8X4), rhs_scale=z_plane[:, cols], start=True, stop=True,
+                out=bank[:, cols],
+                lhsT=words.bitcast(FP8X4),
+                lhsT_scale=plane,
+                rhs=z_words[:, cols].bitcast(FP8X4),
+                rhs_scale=z_plane[:, cols],
+                start=True,
+                stop=True,
             )
-            nc.scalar.activation(scores[t][:, cols], bank[:, cols], ACT.Copy, scale=0.0625)
+            nc.scalar.activation(scores[t][:, cols], bank[:, cols], ACT.Copy, scale=SIXTEENTH)
 
+        half_banks = [new_bank("s_half0"), s_banks[0]]
         for u in range(2):
             nc.vector.quantize_mx(
                 out=z_words[:, half_cols(u)].bitcast(FP8X4),
                 scales=z_plane[:, half_cols(u)],
-                in_=z_rows[u][:].rearrange("p c t -> p (c t)"),
+                in_=z_rounded[u][:].rearrange("p c t -> p (c t)"),
             )
-            for t in order[:1]:
-                score(t, half_cols(u), s_banks[t] if u else psum.tile([P, N], F32, name=f"first_half{t}", tag=f"h_bank{t}"), first_plane[:])
-        rest_plane = new("rest_plane", [P, (PACK - 1) * P], U8, "z_rows1")
-        nc.vector.tensor_copy(rest_plane[:].rearrange("p (t m i) -> p m t i", t=PACK - 1, i=4), by_slot[:, :, 1:, :])
-        for t in order[1:]:
-            score(t, slice(0, N), s_banks[t], rest_plane[:, (t - 1) * P : t * P])
+            score(0, half_cols(u), half_banks[u], first_words[:], first_plane[:])
 
-        out_rows = new("out_rows", [P, N, PACK], BF16)
-        out_dealt = out_0.rearrange("(p t) j -> p t j", t=PACK)
-        pa, lift = {}, {}
+        other_planes = deal("other_planes", cand_bytes, other_slots, U8, "z_rounded1")
+        other_words = deal("other_words", cand_picked, other_slots, U32, "z_half1")
+        for t in SCORE_ORDER[1:]:
+            rows = slice((t - 1) * P, t * P)
+            score(t, slice(0, N), s_banks[t], other_words[:, rows], other_planes[:, rows])
+
+        out_rounded = new("out_rounded", [P, N, SLOTS], BF16)
+        out_slots = out_0.rearrange("(p t) j -> p t j", t=SLOTS)
+        pa, lift = [], []
 
         def fetch(step):
-            t = order[step]
-            pa[t] = new(f"pa{t}", [P, HALF], F32, f"pa_slot{step % 3}")
-            nc.vector.tensor_copy(pa[t][:], scores[t][:].indirect(n3_list[:]))
+            pa.append(new(f"pa{step}", [P, HALF], F32, f"pa_buffer{step % PA_BUFFERS}"))
+            nc.vector.tensor_copy(pa[step][:], scores[SCORE_ORDER[step]][:].indirect(n3_list[:]))
 
         def compare(step):
-            t = order[step]
-            gap = new(f"gap{t}", [P, HALF], F32, f"gap{step}" if step < 2 else f"lift{step - 2}")
-            lift[t] = new(f"lift{t}", [P, HALF], F32, f"lift{step}")
-            nc.vector.tensor_tensor(gap[:], scores[t][:].indirect(n4_list[:]), pa[t][:], ALU.subtract)
-            nc.scalar.activation(lift[t][:], gap[:], ACT.Relu)
+            difference = new(f"difference{step}", [P, HALF], F32, f"lift{step - 2}" if step >= 2 else None)
+            lift.append(new(f"lift{step}", [P, HALF], F32))
+            nc.vector.tensor_tensor(difference[:], scores[SCORE_ORDER[step]][:].indirect(n4_list[:]), pa[step][:], ALU.subtract)
+            nc.scalar.activation(lift[step][:], difference[:], ACT.Relu)
 
         def put_back(step):
-            t = order[step]
-            nc.vector.tensor_tensor(scores[t][:].indirect(n3_list[:]), pa[t][:], lift[t][:], ALU.add)
-            nc.sync.dma_start(out_dealt[:, t, :], scores[t][:])
-            if t < PACK - 2:
-                nc.scalar.copy(out_rows[:, :, t], scores[t][:])
-            elif t == PACK - 2:
-                nc.scalar.copy(out_rows[:, :, t:], scores[t][:].unsqueeze(2).to_broadcast([P, N, 2]))
+            t = SCORE_ORDER[step]
+            nc.vector.tensor_tensor(scores[t][:].indirect(n3_list[:]), pa[step][:], lift[step][:], ALU.add)
+            nc.sync.dma_start(out_slots[:, t, :], scores[t][:])
+            if t < SLOTS - 2:
+                nc.scalar.copy(out_rounded[:, :, t], scores[t][:])
+            elif t == SLOTS - 2:
+                nc.scalar.copy(out_rounded[:, :, t:], scores[t][:].unsqueeze(2).to_broadcast([P, N, 2]))
 
-        fetch(0)
-        fetch(1)
-        compare(0)
-        compare(1)
-        for step in range(PACK):
-            if step + 2 < PACK:
+        for step in range(2):
+            fetch(step)
+        for step in range(2):
+            compare(step)
+        for step in range(SLOTS):
+            if step + 2 < SLOTS:
                 fetch(step + 2)
             put_back(step)
-            if step + 2 < PACK:
+            if step + 2 < SLOTS:
                 compare(step + 2)
 
+        last = SLOTS - 1
         out_words = new("out_words", [P, N], I32)
         out_plane = new("out_plane", [P, N], U8)
-        cut = 384
-        for cols in (slice(0, HALF), slice(HALF, cut)):
-            nc.vector.tensor_copy(out_rows[:, cols, PACK - 1], scores[PACK - 1][:, cols])
-        nc.scalar.copy(out_rows[:, cut:, PACK - 1], scores[PACK - 1][:, cut:])
+        for cols in (half_cols(0), slice(HALF, VECTOR_COLUMNS)):
+            nc.vector.tensor_copy(out_rounded[:, cols, last], scores[last][:, cols])
+        nc.scalar.copy(out_rounded[:, VECTOR_COLUMNS:, last], scores[last][:, VECTOR_COLUMNS:])
         for u in range(2):
             nc.vector.quantize_mx(
                 out=out_words[:, half_cols(u)].bitcast(FP8X4),
                 scales=out_plane[:, half_cols(u)],
-                in_=out_rows[:, half_cols(u), :].rearrange("p c t -> p (c t)"),
+                in_=out_rounded[:, half_cols(u), :].rearrange("p c t -> p (c t)"),
             )
             nc.sync.dma_start(as_words(out_1[0])[:, half_cols(u)], out_words[:, half_cols(u)])
-        for q in range(4):
-            (nc.sync if q == 0 else nc.scalar).dma_start(out_2[0, 4 * q : 4 * q + 4, :].bitcast(I32), out_plane[32 * q : 32 * q + 4, :].bitcast(I32))
+        for q in range(P // QUADRANT):
+            queue = nc.sync if q == 0 else nc.scalar
+            queue.dma_start(
+                out_2[0, PLANE_ROWS * q : PLANE_ROWS * (q + 1), :].bitcast(I32),
+                out_plane[QUADRANT * q : QUADRANT * q + PLANE_ROWS, :].bitcast(I32),
+            )

from contextlib import ExitStack

import concourse.mybir as mybir

F32 = mybir.dt.float32
BF16 = mybir.dt.bfloat16
I32 = mybir.dt.int32
U32 = mybir.dt.uint32
U16 = mybir.dt.uint16
U8 = mybir.dt.uint8
FP8X4 = mybir.dt.float8_e4m3fn_x4
ALU = mybir.AluOpType
ACT = mybir.ActivationFunctionType

P = 128
SLOTS = 4
N = 512
HALF = N // 2
TOKENS = 1024
CODEWORDS = 2048
GROUP = 16
QUADRANT = 32
PLANE_ROWS = 4
LINE = 4
SIXTEENTH = 0.0625
SCORE_ORDER = (0, 2, 1, 3)
PA_BUFFERS = 3
VECTOR_COLUMNS = 384
FLOPS = 2 * 2 * N * N * N


def tile_picked_pqchoppfill_none_po_kernel(
    tc, x_words, x_scales, d_words, d_scales, gs, offs, k1, n1, n2, cand, n3, n4, out_0, out_1, out_2
):
    nc = tc.nc
    with ExitStack() as ctx:
        keep = ctx.enter_context(tc.tile_pool(name="keep", bufs=1))
        psum = ctx.enter_context(tc.psum_pool(name="psum", bufs=1))

        def new(name, shape, dtype, tag=None):
            return keep.tile(shape, dtype, name=name, tag=tag or name, align_bytes=64)

        def new_bank(name, tag=None):
            return psum.tile([P, N], F32, name=name, tag=tag or name)

        def load_list(name, src):
            tile = new(name, list(src.shape), U16)
            nc.sync.dma_start(tile[:], src)
            return tile

        def as_words(codes):
            return codes.rearrange("p n t -> p (n t)").bitcast(I32)

        def half_cols(u):
            return slice(u * HALF, (u + 1) * HALF)

        def half_list(offsets, u):
            return offsets[:, u * HALF // GROUP : (u + 1) * HALF // GROUP]

        def in_list_order(picked):
            return picked.rearrange("p (m i t) -> p m t i", t=SLOTS, i=LINE)

        def in_slot_order(dealt, slots):
            return dealt.rearrange("p (t m i) -> p m t i", t=slots, i=LINE)

        d_bytes = new("d_bytes", [P, CODEWORDS], U8)
        x_bytes = new("x_bytes", [P, TOKENS], U8)
        w_plane = new("w_plane", [P, N], U8)
        nc.vector.memset(d_bytes[:, : CODEWORDS // 2].bitcast(I32), 0)
        nc.gpsimd.memset(d_bytes[:, CODEWORDS // 2 :].bitcast(I32), 0)
        nc.vector.memset(x_bytes[:].bitcast(I32), 0)
        nc.vector.memset(w_plane[:].bitcast(I32), 0)

        h_windows = [new(f"h_window{t}", [P, 2 * N], F32) for t in range(SLOTS)]
        for window in h_windows[:2]:
            nc.vector.memset(window[:, N:].bitcast(I32), 0)

        x_table = new("x_table", [P, TOKENS], I32)
        d_table = new("d_table", [P, CODEWORDS], I32)
        gain = new("gain", [P, SLOTS], F32)
        k1_list = load_list("k1_list", k1)
        offs_list = load_list("offs_list", offs)
        cand_list = load_list("cand_list", cand)
        n1_list = load_list("n1_list", n1)
        for e in range(2):
            nc.sync.dma_start(d_bytes[e:P:GROUP, :].bitcast(I32), d_scales[0, e::2, :].bitcast(I32))
        nc.sync.dma_start(x_table[:], as_words(x_words[0]))
        nc.sync.dma_start(d_table[:], as_words(d_words[0]))
        for q in range(P // QUADRANT):
            nc.sync.dma_start(
                x_bytes[QUADRANT * q : QUADRANT * q + PLANE_ROWS, :].bitcast(I32),
                x_scales[0, PLANE_ROWS * q : PLANE_ROWS * (q + 1), :].bitcast(I32),
            )
        nc.sync.dma_start(gain[:], gs.rearrange("(p t) o -> p (t o)", t=SLOTS))
        n2_list = load_list("n2_list", n2)
        n3_list = load_list("n3_list", n3)
        n4_list = load_list("n4_list", n4)

        warm = new("warm", [P, SLOTS], F32)
        nc.scalar.activation(warm[:], gain[:], ACT.Tanh)

        def pick(name, window, offsets, dtype, tag=None):
            picked = new(name, [P, GROUP * offsets.shape[1]], dtype, tag)
            nc.vector.tensor_copy(picked[:], window.indirect(offsets))
            return picked

        def deal(name, picked, slots, dtype, tag=None):
            count = slots.stop - slots.start
            dealt = new(name, [P, count * P], dtype, tag)
            nc.vector.tensor_copy(in_slot_order(dealt[:], count), in_list_order(picked[:])[:, :, slots, :])
            return dealt

        every_slot, first_slot, other_slots = slice(0, SLOTS), slice(0, 1), slice(1, SLOTS)

        w_bytes = deal("w_bytes", pick("w_bytes_picked", d_bytes[:], k1_list[:], U8), every_slot, U8)
        for c in range(PLANE_ROWS):
            row = GROUP * (c // 2) + c % 2
            nc.sync.dma_start(w_plane[c:P:QUADRANT, :].bitcast(I32), w_bytes[row:P:QUADRANT, :].bitcast(I32))
        token_words = pick("token_words", x_table[:].bitcast(U32), offs_list[:], U32)
        w_picked = pick("w_picked", d_table[:].bitcast(U32), k1_list[:], U32)
        token_planes = [pick("token_plane0", x_bytes[:], half_list(offs_list, 0), U8)]
        w_words = deal("w_words", w_picked, every_slot, U32)
        token_planes.append(pick("token_plane1", x_bytes[:], half_list(offs_list, 1), U8))

        h_plain = [new("h_plain0", [P, N], F32)[:], h_windows[2][:, N:], h_windows[3][:, N:], new("h_plain3", [P, N], F32)[:]]

        def layer_product(t, u, bank):
            rows = slice(t * P, (t + 1) * P)
            nc.tensor.matmul_mx(
                out=bank[:, half_cols(u)],
                lhsT=w_words[:, rows].bitcast(FP8X4),
                lhsT_scale=w_plane[:, rows],
                rhs=token_words[:, half_cols(u)].bitcast(FP8X4),
                rhs_scale=token_planes[u][:],
                start=True,
                stop=True,
            )

        def copy_h(t, cols, bank):
            nc.scalar.activation(h_windows[t][:, cols], bank[:, cols], ACT.Copy, scale=SIXTEENTH)
            nc.scalar.activation(h_plain[t][:, cols], bank[:, cols], ACT.Copy, scale=SIXTEENTH)

        for u in range(2):
            bank = new_bank(f"h_half{u}", f"s_bank{u + 2}")
            layer_product(0, u, bank)
            copy_h(0, half_cols(u), bank)
        for t in range(1, SLOTS):
            bank = new_bank(f"h_bank{t}")
            for u in range(2):
                layer_product(t, u, bank)
            copy_h(t, slice(0, N), bank)

        cand_picked = pick("cand_picked", x_table[:].bitcast(U32), cand_list[:], U32, "w_bytes")
        first_words = deal("first_words", cand_picked, first_slot, U32)

        states, tanh_windows, gained = [], [], []

        def apply_gain(t, cols):
            nc.scalar.activation(gained[t][:, cols], states[t][:, cols], ACT.Copy, scale=gain[:, t : t + 1])

        for t in range(SLOTS):
            states.append(new(f"state{t}", [P, N], F32))
            nc.vector.tensor_tensor(states[t][:], h_windows[t][:].indirect(n1_list[:]), h_plain[t], ALU.add)
            tanh_windows.append(new(f"tanh_window{t}", [P, N], F32))
            gained.append(new(f"gained{t}", [P, N], F32))
            nc.scalar.activation(tanh_windows[t][:], states[t][:], ACT.Tanh)
            apply_gain(t, slice(0, N) if t == 0 else half_cols(0))
        for t in range(1, SLOTS):
            apply_gain(t, half_cols(1))

        z_halves = [new(f"z_half{u}", [P, SLOTS, HALF], F32) for u in range(2)]
        z_rounded = [new(f"z_rounded{u}", [P, HALF, SLOTS], BF16) for u in range(2)]

        def make_z(u, t):
            nc.vector.tensor_tensor(
                z_halves[u][:, t, :], tanh_windows[t][:].indirect(half_list(n2_list, u)), gained[t][:, half_cols(u)], ALU.mult
            )

        for u in range(2):
            make_z(u, 0)
        for u in range(2):
            for t in range(1, SLOTS):
                make_z(u, t)
            nc.scalar.copy(
                z_rounded[u][:].rearrange("p (c i) t -> p c t i", i=LINE),
                z_halves[u][:].rearrange("p t (c i) -> p c t i", i=LINE),
            )

        cand_bytes = pick("cand_bytes", x_bytes[:], cand_list[:], U8, f"tanh_window{SLOTS - 1}")
        first_plane = deal("first_plane", cand_bytes, first_slot, U8)

        s_banks = [new_bank(f"s_bank{t}") for t in range(SLOTS)]
        scores = [new(f"scores{t}", [P, N], F32) for t in range(SLOTS)]
        z_words = new("z_words", [P, N], U32)
        z_plane = new("z_plane", [P, N], U8)

        def score(t, cols, bank, words, plane):
            nc.tensor.matmul_mx(
                out=bank[:, cols],
                lhsT=words.bitcast(FP8X4),
                lhsT_scale=plane,
                rhs=z_words[:, cols].bitcast(FP8X4),
                rhs_scale=z_plane[:, cols],
                start=True,
                stop=True,
            )
            nc.scalar.activation(scores[t][:, cols], bank[:, cols], ACT.Copy, scale=SIXTEENTH)

        half_banks = [new_bank("s_half0"), s_banks[0]]
        for u in range(2):
            nc.vector.quantize_mx(
                out=z_words[:, half_cols(u)].bitcast(FP8X4),
                scales=z_plane[:, half_cols(u)],
                in_=z_rounded[u][:].rearrange("p c t -> p (c t)"),
            )
            score(0, half_cols(u), half_banks[u], first_words[:], first_plane[:])

        other_planes = deal("other_planes", cand_bytes, other_slots, U8, "z_rounded1")
        other_words = deal("other_words", cand_picked, other_slots, U32, "z_half1")
        for t in SCORE_ORDER[1:]:
            rows = slice((t - 1) * P, t * P)
            score(t, slice(0, N), s_banks[t], other_words[:, rows], other_planes[:, rows])

        out_rounded = new("out_rounded", [P, N, SLOTS], BF16)
        out_slots = out_0.rearrange("(p t) j -> p t j", t=SLOTS)
        pa, lift = [], []

        def fetch(step):
            pa.append(new(f"pa{step}", [P, HALF], F32, f"pa_buffer{step % PA_BUFFERS}"))
            nc.vector.tensor_copy(pa[step][:], scores[SCORE_ORDER[step]][:].indirect(n3_list[:]))

        def compare(step):
            difference = new(f"difference{step}", [P, HALF], F32, f"lift{step - 2}" if step >= 2 else None)
            lift.append(new(f"lift{step}", [P, HALF], F32))
            nc.vector.tensor_tensor(difference[:], scores[SCORE_ORDER[step]][:].indirect(n4_list[:]), pa[step][:], ALU.subtract)
            nc.scalar.activation(lift[step][:], difference[:], ACT.Relu)

        def put_back(step):
            t = SCORE_ORDER[step]
            nc.vector.tensor_tensor(scores[t][:].indirect(n3_list[:]), pa[step][:], lift[step][:], ALU.add)
            nc.sync.dma_start(out_slots[:, t, :], scores[t][:])
            if t < SLOTS - 2:
                nc.scalar.copy(out_rounded[:, :, t], scores[t][:])
            elif t == SLOTS - 2:
                nc.scalar.copy(out_rounded[:, :, t:], scores[t][:].unsqueeze(2).to_broadcast([P, N, 2]))

        for step in range(2):
            fetch(step)
        for step in range(2):
            compare(step)
        for step in range(SLOTS):
            if step + 2 < SLOTS:
                fetch(step + 2)
            put_back(step)
            if step + 2 < SLOTS:
                compare(step + 2)

        last = SLOTS - 1
        out_words = new("out_words", [P, N], I32)
        out_plane = new("out_plane", [P, N], U8)
        for cols in (half_cols(0), slice(HALF, VECTOR_COLUMNS)):
            nc.vector.tensor_copy(out_rounded[:, cols, last], scores[last][:, cols])
        nc.scalar.copy(out_rounded[:, VECTOR_COLUMNS:, last], scores[last][:, VECTOR_COLUMNS:])
        for u in range(2):
            nc.vector.quantize_mx(
                out=out_words[:, half_cols(u)].bitcast(FP8X4),
                scales=out_plane[:, half_cols(u)],
                in_=out_rounded[:, half_cols(u), :].rearrange("p c t -> p (c t)"),
            )
            nc.sync.dma_start(as_words(out_1[0])[:, half_cols(u)], out_words[:, half_cols(u)])
        for q in range(P // QUADRANT):
            queue = nc.sync if q == 0 else nc.scalar
            queue.dma_start(
                out_2[0, PLANE_ROWS * q : PLANE_ROWS * (q + 1), :].bitcast(I32),
                out_plane[QUADRANT * q : QUADRANT * q + PLANE_ROWS, :].bitcast(I32),
            )
